import numpy as np
import ml_dtypes

BF16 = ml_dtypes.bfloat16


def bf(x):
    return np.asarray(x, np.float32).astype(BF16)


def f32(x):
    return np.asarray(x, np.float32)


def f64(x):
    return np.asarray(x).astype(np.float64)


def striped(idx):
    return np.tile(idx.reshape(-1, 16).T, (8, 1))


def rows(idx, k):
    return np.tile(idx, (k, 1))


def look(tab, idx):
    return np.take_along_axis(f64(tab), rows(idx, len(tab)), axis=1)


K, S, V, N = 256, 2048, 512, 512


def setup_inputs():
    return {"tab": f32(np.random.standard_normal((2, K, S))), "y": f32(np.random.standard_normal((K, V))), "offs": striped(np.random.permutation(S)[:N])}


def reference(tab, y, offs):
    idx = offs[:16].T.reshape(-1)
    x = (look(tab[0], idx) * f64(y)) * (np.tanh(look(tab[1], idx)))
    return x

@@ -1,0 +1,45 @@
+import concourse.mybir as mybir
+
+F32, U16 = mybir.dt.float32, mybir.dt.uint16
+MULT = mybir.AluOpType.mult
+TANH = mybir.ActivationFunctionType.Tanh
+P = 128
+
+
+def tile_lookup_vg_multanh_out_kernel(tc, tab, y, offs, out):
+    nc = tc.nc
+    rows, picked = y.shape
+    places = tab.shape[2]
+    blocks = rows // P
+    table_rows = tab.rearrange("t (p b) s -> t b p s", b=blocks)
+    stream_rows = y.rearrange("(p b) v -> p b v", b=blocks)
+    out_rows = out.rearrange("(p b) v -> b p v", b=blocks)
+
+    with tc.tile_pool(name="held", bufs=1) as held, tc.tile_pool(name="work", bufs=2) as work:
+        offsets = held.tile([P, picked // 16], U16, name="offsets")
+        nc.sync.dma_start(offsets[:], offs)
+
+        gates = [held.tile([P, places], F32, name=f"gates{b}") for b in range(blocks)]
+        stream = held.tile([P, blocks, picked], F32, name="stream")
+        values = [held.tile([P, places], F32, name=f"values{b}") for b in range(blocks)]
+        for b in range(blocks):
+            nc.sync.dma_start(gates[b][:], table_rows[1, b])
+        nc.sync.dma_start(stream[:], stream_rows)
+        for b in range(blocks):
+            nc.sync.dma_start(values[b][:], table_rows[0, b])
+
+        gated_stream = held.tile([P, blocks, picked], F32, name="gated_stream")
+        for b in range(blocks):
+            gate = work.tile([P, picked], F32, name="gate")
+            nc.scalar.activation(gate[:], gates[b][:].indirect(offsets[:]), TANH)
+            nc.vector.tensor_tensor(gated_stream[:, b], stream[:, b], gate[:], MULT)
+
+        for b in range(blocks):
+            result = work.tile([P, picked], F32, name="result")
+            for k in range(2):
+                piece = slice(k * picked // 2, (k + 1) * picked // 2)
+                list_columns = offsets[:, k * picked // 32 : (k + 1) * picked // 32]
+                nc.vector.tensor_tensor(
+                    result[:, piece], values[b][:].indirect(list_columns), gated_stream[:, b, piece], MULT
+                )
+                nc.sync.dma_start(out_rows[b, :, piece], result[:, piece])

@@ -22,9 +22,9 @@ def tile_lookup_vg_multanh_out_kernel(tc, tab, y, offs, out):
         gates = [held.tile([P, places], F32, name=f"gates{b}") for b in range(blocks)]
         stream = held.tile([P, blocks, picked], F32, name="stream")
         values = [held.tile([P, places], F32, name=f"values{b}") for b in range(blocks)]
-        for b in range(blocks):
-            nc.sync.dma_start(gates[b][:], table_rows[1, b])
-        nc.sync.dma_start(stream[:], stream_rows)
+        nc.scalar.dma_start(gates[0][:], table_rows[1, 0])
+        nc.sync.dma_start(gates[1][:], table_rows[1, 1])
+        nc.scalar.dma_start(stream[:], stream_rows)
         for b in range(blocks):
             nc.sync.dma_start(values[b][:], table_rows[0, b])
 

@@ -4,6 +4,7 @@ F32, U16 = mybir.dt.float32, mybir.dt.uint16
 MULT = mybir.AluOpType.mult
 TANH = mybir.ActivationFunctionType.Tanh
 P = 128
+GROUP = 16
 
 
 def tile_lookup_vg_multanh_out_kernel(tc, tab, y, offs, out):
@@ -16,12 +17,12 @@ def tile_lookup_vg_multanh_out_kernel(tc, tab, y, offs, out):
     out_rows = out.rearrange("(p b) v -> b p v", b=blocks)
 
     with tc.tile_pool(name="held", bufs=1) as held, tc.tile_pool(name="work", bufs=2) as work:
-        offsets = held.tile([P, picked // 16], U16, name="offsets")
-        nc.sync.dma_start(offsets[:], offs)
-
+        offsets = held.tile([P, picked // GROUP], U16, name="offsets")
         gates = [held.tile([P, places], F32, name=f"gates{b}") for b in range(blocks)]
         stream = held.tile([P, blocks, picked], F32, name="stream")
         values = [held.tile([P, places], F32, name=f"values{b}") for b in range(blocks)]
+
+        nc.sync.dma_start(offsets[:], offs)
         nc.scalar.dma_start(gates[0][:], table_rows[1, 0])
         nc.sync.dma_start(gates[1][:], table_rows[1, 1])
         nc.scalar.dma_start(stream[:], stream_rows)
@@ -34,12 +35,12 @@ def tile_lookup_vg_multanh_out_kernel(tc, tab, y, offs, out):
             nc.scalar.activation(gate[:], gates[b][:].indirect(offsets[:]), TANH)
             nc.vector.tensor_tensor(gated_stream[:, b], stream[:, b], gate[:], MULT)
 
+        cuts = [(0, picked // 2, picked), (0, 5 * picked // 8, picked)]
         for b in range(blocks):
             result = work.tile([P, picked], F32, name="result")
-            for k in range(2):
-                piece = slice(k * picked // 2, (k + 1) * picked // 2)
-                list_columns = offsets[:, k * picked // 32 : (k + 1) * picked // 32]
+            for k, (first, last) in enumerate(zip(cuts[b], cuts[b][1:])):
+                list_columns = offsets[:, first // GROUP : last // GROUP]
                 nc.vector.tensor_tensor(
-                    result[:, piece], values[b][:].indirect(list_columns), gated_stream[:, b, piece], MULT
+                    result[:, first:last], values[b][:].indirect(list_columns), gated_stream[:, b, first:last], MULT
                 )
-                nc.sync.dma_start(out_rows[b, :, piece], result[:, piece])
+                nc.sync.dma_start(out_rows[b, :, first:last], result[:, first:last])

@@ -23,11 +23,11 @@ def tile_lookup_vg_multanh_out_kernel(tc, tab, y, offs, out):
         values = [held.tile([P, places], F32, name=f"values{b}") for b in range(blocks)]
 
         nc.sync.dma_start(offsets[:], offs)
-        nc.scalar.dma_start(gates[0][:], table_rows[1, 0])
-        nc.sync.dma_start(gates[1][:], table_rows[1, 1])
-        nc.scalar.dma_start(stream[:], stream_rows)
+        nc.sync.dma_start(stream[:], stream_rows)
         for b in range(blocks):
-            nc.sync.dma_start(values[b][:], table_rows[0, b])
+            nc.gpsimd.dma_start(gates[b][:], table_rows[1, b])
+        for b in range(blocks):
+            nc.gpsimd.dma_start(values[b][:], table_rows[0, b])
 
         gated_stream = held.tile([P, blocks, picked], F32, name="gated_stream")
         for b in range(blocks):

@@ -24,23 +24,21 @@ def tile_lookup_vg_multanh_out_kernel(tc, tab, y, offs, out):
 
         nc.sync.dma_start(offsets[:], offs)
         nc.sync.dma_start(stream[:], stream_rows)
-        for b in range(blocks):
-            nc.gpsimd.dma_start(gates[b][:], table_rows[1, b])
+        nc.gpsimd.dma_start(gates[0][:], table_rows[1, 0])
+        nc.sync.dma_start(gates[1][:], table_rows[1, 1])
         for b in range(blocks):
             nc.gpsimd.dma_start(values[b][:], table_rows[0, b])
 
-        gated_stream = held.tile([P, blocks, picked], F32, name="gated_stream")
+        cuts = [(0, picked), (0, 5 * picked // 8, picked)]
         for b in range(blocks):
             gate = work.tile([P, picked], F32, name="gate")
             nc.scalar.activation(gate[:], gates[b][:].indirect(offsets[:]), TANH)
-            nc.vector.tensor_tensor(gated_stream[:, b], stream[:, b], gate[:], MULT)
-
-        cuts = [(0, picked // 2, picked), (0, 5 * picked // 8, picked)]
-        for b in range(blocks):
+            gated_stream = work.tile([P, picked], F32, name="gated_stream")
+            nc.vector.tensor_tensor(gated_stream[:], stream[:, b], gate[:], MULT)
             result = work.tile([P, picked], F32, name="result")
-            for k, (first, last) in enumerate(zip(cuts[b], cuts[b][1:])):
+            for first, last in zip(cuts[b], cuts[b][1:]):
                 list_columns = offsets[:, first // GROUP : last // GROUP]
                 nc.vector.tensor_tensor(
-                    result[:, first:last], values[b][:].indirect(list_columns), gated_stream[:, b, first:last], MULT
+                    result[:, first:last], values[b][:].indirect(list_columns), gated_stream[:, first:last], MULT
                 )
                 nc.sync.dma_start(out_rows[b, :, first:last], result[:, first:last])

@@ -23,9 +23,9 @@ def tile_lookup_vg_multanh_out_kernel(tc, tab, y, offs, out):
         values = [held.tile([P, places], F32, name=f"values{b}") for b in range(blocks)]
 
         nc.sync.dma_start(offsets[:], offs)
-        nc.sync.dma_start(stream[:], stream_rows)
-        nc.gpsimd.dma_start(gates[0][:], table_rows[1, 0])
-        nc.sync.dma_start(gates[1][:], table_rows[1, 1])
+        nc.sync.dma_start(gates[0][:], table_rows[1, 0])
+        nc.gpsimd.dma_start(gates[1][:], table_rows[1, 1])
+        nc.gpsimd.dma_start(stream[:], stream_rows)
         for b in range(blocks):
             nc.gpsimd.dma_start(values[b][:], table_rows[0, b])
 

@@ -29,6 +29,7 @@ def tile_lookup_vg_multanh_out_kernel(tc, tab, y, offs, out):
         for b in range(blocks):
             nc.gpsimd.dma_start(values[b][:], table_rows[0, b])
 
+        store_queues = [nc.scalar, nc.sync]
         cuts = [(0, picked), (0, 5 * picked // 8, picked)]
         for b in range(blocks):
             gate = work.tile([P, picked], F32, name="gate")
@@ -41,4 +42,4 @@ def tile_lookup_vg_multanh_out_kernel(tc, tab, y, offs, out):
                 nc.vector.tensor_tensor(
                     result[:, first:last], values[b][:].indirect(list_columns), gated_stream[:, first:last], MULT
                 )
-                nc.sync.dma_start(out_rows[b, :, first:last], result[:, first:last])
+                store_queues[b].dma_start(out_rows[b, :, first:last], result[:, first:last])

@@ -22,8 +22,8 @@ def tile_lookup_vg_multanh_out_kernel(tc, tab, y, offs, out):
         stream = held.tile([P, blocks, picked], F32, name="stream")
         values = [held.tile([P, places], F32, name=f"values{b}") for b in range(blocks)]
 
-        nc.sync.dma_start(offsets[:], offs)
         nc.sync.dma_start(gates[0][:], table_rows[1, 0])
+        nc.sync.dma_start(offsets[:], offs)
         nc.gpsimd.dma_start(gates[1][:], table_rows[1, 1])
         nc.gpsimd.dma_start(stream[:], stream_rows)
         for b in range(blocks):

@@ -22,24 +22,26 @@ def tile_lookup_vg_multanh_out_kernel(tc, tab, y, offs, out):
         stream = held.tile([P, blocks, picked], F32, name="stream")
         values = [held.tile([P, places], F32, name=f"values{b}") for b in range(blocks)]
 
-        nc.sync.dma_start(gates[0][:], table_rows[1, 0])
+        nc.sync.dma_start(gates[1][:], table_rows[1, 1])
         nc.sync.dma_start(offsets[:], offs)
-        nc.gpsimd.dma_start(gates[1][:], table_rows[1, 1])
+        nc.gpsimd.dma_start(gates[0][:], table_rows[1, 0])
         nc.gpsimd.dma_start(stream[:], stream_rows)
         for b in range(blocks):
             nc.gpsimd.dma_start(values[b][:], table_rows[0, b])
 
+        gated_stream = held.tile([P, blocks, picked], F32, name="gated_stream")
+        for b in reversed(range(blocks)):
+            gate = work.tile([P, picked], F32, name="gate")
+            nc.scalar.activation(gate[:], gates[b][:].indirect(offsets[:]), TANH)
+            nc.vector.tensor_tensor(gated_stream[:, b], stream[:, b], gate[:], MULT)
+
         store_queues = [nc.scalar, nc.sync]
         cuts = [(0, picked), (0, 5 * picked // 8, picked)]
         for b in range(blocks):
-            gate = work.tile([P, picked], F32, name="gate")
-            nc.scalar.activation(gate[:], gates[b][:].indirect(offsets[:]), TANH)
-            gated_stream = work.tile([P, picked], F32, name="gated_stream")
-            nc.vector.tensor_tensor(gated_stream[:], stream[:, b], gate[:], MULT)
             result = work.tile([P, picked], F32, name="result")
             for first, last in zip(cuts[b], cuts[b][1:]):
                 list_columns = offsets[:, first // GROUP : last // GROUP]
                 nc.vector.tensor_tensor(
-                    result[:, first:last], values[b][:].indirect(list_columns), gated_stream[:, first:last], MULT
+                    result[:, first:last], values[b][:].indirect(list_columns), gated_stream[:, b, first:last], MULT
                 )
                 store_queues[b].dma_start(out_rows[b, :, first:last], result[:, first:last])

@@ -36,7 +36,7 @@ def tile_lookup_vg_multanh_out_kernel(tc, tab, y, offs, out):
             nc.vector.tensor_tensor(gated_stream[:, b], stream[:, b], gate[:], MULT)
 
         store_queues = [nc.scalar, nc.sync]
-        cuts = [(0, picked), (0, 5 * picked // 8, picked)]
+        cuts = [(0, picked), (0, 9 * picked // 16, picked)]
         for b in range(blocks):
             result = work.tile([P, picked], F32, name="result")
             for first, last in zip(cuts[b], cuts[b][1:]):

@@ -5,6 +5,7 @@ MULT = mybir.AluOpType.mult
 TANH = mybir.ActivationFunctionType.Tanh
 P = 128
 GROUP = 16
+BURST = 256
 
 
 def tile_lookup_vg_multanh_out_kernel(tc, tab, y, offs, out):
@@ -18,9 +19,9 @@ def tile_lookup_vg_multanh_out_kernel(tc, tab, y, offs, out):
 
     with tc.tile_pool(name="held", bufs=1) as held, tc.tile_pool(name="work", bufs=2) as work:
         offsets = held.tile([P, picked // GROUP], U16, name="offsets")
-        gates = [held.tile([P, places], F32, name=f"gates{b}") for b in range(blocks)]
-        stream = held.tile([P, blocks, picked], F32, name="stream")
-        values = [held.tile([P, places], F32, name=f"values{b}") for b in range(blocks)]
+        gates = [held.tile([P, places], F32, name=f"gates{b}", align_bytes=BURST) for b in range(blocks)]
+        stream = held.tile([P, blocks, picked], F32, name="stream", align_bytes=BURST)
+        values = [held.tile([P, places], F32, name=f"values{b}", align_bytes=BURST) for b in range(blocks)]
 
         nc.sync.dma_start(gates[1][:], table_rows[1, 1])
         nc.sync.dma_start(offsets[:], offs)
@@ -38,7 +39,7 @@ def tile_lookup_vg_multanh_out_kernel(tc, tab, y, offs, out):
         store_queues = [nc.scalar, nc.sync]
         cuts = [(0, picked), (0, 9 * picked // 16, picked)]
         for b in range(blocks):
-            result = work.tile([P, picked], F32, name="result")
+            result = work.tile([P, picked], F32, name="result", align_bytes=BURST)
             for first, last in zip(cuts[b], cuts[b][1:]):
                 list_columns = offsets[:, first // GROUP : last // GROUP]
                 nc.vector.tensor_tensor(

@@ -37,7 +37,7 @@ def tile_lookup_vg_multanh_out_kernel(tc, tab, y, offs, out):
             nc.vector.tensor_tensor(gated_stream[:, b], stream[:, b], gate[:], MULT)
 
         store_queues = [nc.scalar, nc.sync]
-        cuts = [(0, picked), (0, 9 * picked // 16, picked)]
+        cuts = [(0, picked), (0, 5 * picked // 8, picked)]
         for b in range(blocks):
             result = work.tile([P, picked], F32, name="result", align_bytes=BURST)
             for first, last in zip(cuts[b], cuts[b][1:]):

@@ -13,36 +13,48 @@ def tile_lookup_vg_multanh_out_kernel(tc, tab, y, offs, out):
     rows, picked = y.shape
     places = tab.shape[2]
     blocks = rows // P
-    table_rows = tab.rearrange("t (p b) s -> t b p s", b=blocks)
+    table_rows = tab.rearrange("t (p b) s -> t p b s", b=blocks)
     stream_rows = y.rearrange("(p b) v -> p b v", b=blocks)
     out_rows = out.rearrange("(p b) v -> b p v", b=blocks)
 
-    with tc.tile_pool(name="held", bufs=1) as held, tc.tile_pool(name="work", bufs=2) as work:
+    with tc.tile_pool(name="held", bufs=1) as held, tc.tile_pool(name="reused", bufs=1) as reused:
         offsets = held.tile([P, picked // GROUP], U16, name="offsets")
-        gates = [held.tile([P, places], F32, name=f"gates{b}", align_bytes=BURST) for b in range(blocks)]
+        both_gates = reused.tile([P, blocks, places], F32, name="both_gates", align_bytes=BURST, offset=0)
         stream = held.tile([P, blocks, picked], F32, name="stream", align_bytes=BURST)
         values = [held.tile([P, places], F32, name=f"values{b}", align_bytes=BURST) for b in range(blocks)]
 
-        nc.sync.dma_start(gates[1][:], table_rows[1, 1])
+        nc.sync.dma_start(both_gates[:], table_rows[1])
         nc.sync.dma_start(offsets[:], offs)
-        nc.gpsimd.dma_start(gates[0][:], table_rows[1, 0])
-        nc.gpsimd.dma_start(stream[:], stream_rows)
+        nc.sync.dma_start(stream[:], stream_rows)
         for b in range(blocks):
-            nc.gpsimd.dma_start(values[b][:], table_rows[0, b])
+            nc.sync.dma_start(values[b][:], table_rows[0, :, b])
 
+        gates = [held.tile([P, places], F32, name=f"gates{b}") for b in range(blocks)]
+        third = 11 * places // 32
+        nc.vector.tensor_copy(gates[0][:, third:], both_gates[:, 0, third:])
+        nc.scalar.copy(gates[0][:, :third], both_gates[:, 0, :third])
+        nc.vector.tensor_copy(gates[1][:], both_gates[:, 1])
+
+        cut = 5 * picked // 8
+        pieces = [(0, 0, picked), (1, 0, cut), (1, cut, picked)]
         gated_stream = held.tile([P, blocks, picked], F32, name="gated_stream")
-        for b in reversed(range(blocks)):
-            gate = work.tile([P, picked], F32, name="gate")
-            nc.scalar.activation(gate[:], gates[b][:].indirect(offsets[:]), TANH)
-            nc.vector.tensor_tensor(gated_stream[:, b], stream[:, b], gate[:], MULT)
+        gate_tiles = [
+            held.tile([P, picked], F32, name="gate0"),
+            reused.tile([P, cut], F32, name="gate1", offset=0),
+            reused.tile([P, picked - cut], F32, name="gate2", offset=picked * 4),
+        ]
+        for gate, (b, first, last) in zip(gate_tiles, pieces):
+            nc.scalar.activation(gate[:], gates[b][:].indirect(offsets[:, first // GROUP : last // GROUP]), TANH)
+            nc.vector.tensor_tensor(gated_stream[:, b, first:last], stream[:, b, first:last], gate[:], MULT)
 
+        results = [
+            reused.tile([P, picked], F32, name="result0", offset=0),
+            held.tile([P, picked], F32, name="result1", align_bytes=BURST),
+        ]
         store_queues = [nc.scalar, nc.sync]
-        cuts = [(0, picked), (0, 5 * picked // 8, picked)]
-        for b in range(blocks):
-            result = work.tile([P, picked], F32, name="result", align_bytes=BURST)
-            for first, last in zip(cuts[b], cuts[b][1:]):
-                list_columns = offsets[:, first // GROUP : last // GROUP]
-                nc.vector.tensor_tensor(
-                    result[:, first:last], values[b][:].indirect(list_columns), gated_stream[:, b, first:last], MULT
-                )
-                store_queues[b].dma_start(out_rows[b, :, first:last], result[:, first:last])
+        for b, first, last in pieces:
+            list_columns = offsets[:, first // GROUP : last // GROUP]
+            nc.vector.tensor_tensor(
+                results[b][:, first:last], values[b][:].indirect(list_columns), gated_stream[:, b, first:last], MULT
+            )
+            store_queues[b].dma_start(out_rows[b, :, first:last], results[b][:, first:last])

@@ -37,24 +37,33 @@ def tile_lookup_vg_multanh_out_kernel(tc, tab, y, offs, out):
 
         cut = 5 * picked // 8
         pieces = [(0, 0, picked), (1, 0, cut), (1, cut, picked)]
-        gated_stream = held.tile([P, blocks, picked], F32, name="gated_stream")
+        lists = [offsets[:, first // GROUP : last // GROUP] for b, first, last in pieces]
         gate_tiles = [
             held.tile([P, picked], F32, name="gate0"),
             reused.tile([P, cut], F32, name="gate1", offset=0),
             reused.tile([P, picked - cut], F32, name="gate2", offset=picked * 4),
         ]
-        for gate, (b, first, last) in zip(gate_tiles, pieces):
-            nc.scalar.activation(gate[:], gates[b][:].indirect(offsets[:, first // GROUP : last // GROUP]), TANH)
-            nc.vector.tensor_tensor(gated_stream[:, b, first:last], stream[:, b, first:last], gate[:], MULT)
-
-        results = [
-            reused.tile([P, picked], F32, name="result0", offset=0),
-            held.tile([P, picked], F32, name="result1", align_bytes=BURST),
+        gated_tiles = [
+            held.tile([P, picked], F32, name="gated0"),
+            held.tile([P, cut], F32, name="gated1"),
+            reused.tile([P, picked - cut], F32, name="gated2", offset=0),
         ]
+        results = [held.tile([P, picked], F32, name=f"result{b}", align_bytes=BURST) for b in range(blocks)]
         store_queues = [nc.scalar, nc.sync]
-        for b, first, last in pieces:
-            list_columns = offsets[:, first // GROUP : last // GROUP]
-            nc.vector.tensor_tensor(
-                results[b][:, first:last], values[b][:].indirect(list_columns), gated_stream[:, b, first:last], MULT
-            )
+
+        def gate_stream(n):
+            b, first, last = pieces[n]
+            nc.scalar.activation(gate_tiles[n][:], gates[b][:].indirect(lists[n]), TANH)
+            nc.vector.tensor_tensor(gated_tiles[n][:], stream[:, b, first:last], gate_tiles[n][:], MULT)
+
+        def look_up(n):
+            b, first, last = pieces[n]
+            nc.vector.tensor_tensor(results[b][:, first:last], values[b][:].indirect(lists[n]), gated_tiles[n][:], MULT)
             store_queues[b].dma_start(out_rows[b, :, first:last], results[b][:, first:last])
+
+        gate_stream(0)
+        look_up(0)
+        gate_stream(1)
+        gate_stream(2)
+        look_up(1)
+        look_up(2)

@@ -49,7 +49,6 @@ def tile_lookup_vg_multanh_out_kernel(tc, tab, y, offs, out):
             reused.tile([P, picked - cut], F32, name="gated2", offset=0),
         ]
         results = [held.tile([P, picked], F32, name=f"result{b}", align_bytes=BURST) for b in range(blocks)]
-        store_queues = [nc.scalar, nc.sync]
 
         def gate_stream(n):
             b, first, last = pieces[n]
@@ -59,7 +58,7 @@ def tile_lookup_vg_multanh_out_kernel(tc, tab, y, offs, out):
         def look_up(n):
             b, first, last = pieces[n]
             nc.vector.tensor_tensor(results[b][:, first:last], values[b][:].indirect(lists[n]), gated_tiles[n][:], MULT)
-            store_queues[b].dma_start(out_rows[b, :, first:last], results[b][:, first:last])
+            nc.sync.dma_start(out_rows[b, :, first:last], results[b][:, first:last])
 
         gate_stream(0)
         look_up(0)

@@ -6,6 +6,7 @@ TANH = mybir.ActivationFunctionType.Tanh
 P = 128
 GROUP = 16
 BURST = 256
+VALUES, GATES = 0, 1
 
 
 def tile_lookup_vg_multanh_out_kernel(tc, tab, y, offs, out):
@@ -13,56 +14,47 @@ def tile_lookup_vg_multanh_out_kernel(tc, tab, y, offs, out):
     rows, picked = y.shape
     places = tab.shape[2]
     blocks = rows // P
-    table_rows = tab.rearrange("t (p b) s -> t p b s", b=blocks)
+    table_rows = tab.rearrange("t (p b) s -> b p t s", b=blocks)
     stream_rows = y.rearrange("(p b) v -> p b v", b=blocks)
     out_rows = out.rearrange("(p b) v -> b p v", b=blocks)
 
     with tc.tile_pool(name="held", bufs=1) as held, tc.tile_pool(name="reused", bufs=1) as reused:
         offsets = held.tile([P, picked // GROUP], U16, name="offsets")
-        both_gates = reused.tile([P, blocks, places], F32, name="both_gates", align_bytes=BURST, offset=0)
+        first_tables = held.tile([P, 2, places], F32, name="first_tables", align_bytes=BURST)
         stream = held.tile([P, blocks, picked], F32, name="stream", align_bytes=BURST)
-        values = [held.tile([P, places], F32, name=f"values{b}", align_bytes=BURST) for b in range(blocks)]
+        last_gates = held.tile([P, places], F32, name="last_gates", align_bytes=BURST)
+        last_values = held.tile([P, places], F32, name="last_values", align_bytes=BURST)
 
-        nc.sync.dma_start(both_gates[:], table_rows[1])
+        nc.sync.dma_start(first_tables[:], table_rows[0])
         nc.sync.dma_start(offsets[:], offs)
         nc.sync.dma_start(stream[:], stream_rows)
-        for b in range(blocks):
-            nc.sync.dma_start(values[b][:], table_rows[0, :, b])
+        nc.sync.dma_start(last_gates[:], table_rows[1, :, GATES])
+        nc.sync.dma_start(last_values[:], table_rows[1, :, VALUES])
 
-        gates = [held.tile([P, places], F32, name=f"gates{b}") for b in range(blocks)]
+        first_values = held.tile([P, places], F32, name="first_values")
+        first_gates = held.tile([P, places], F32, name="first_gates")
         third = 11 * places // 32
-        nc.vector.tensor_copy(gates[0][:, third:], both_gates[:, 0, third:])
-        nc.scalar.copy(gates[0][:, :third], both_gates[:, 0, :third])
-        nc.vector.tensor_copy(gates[1][:], both_gates[:, 1])
+        nc.vector.tensor_copy(first_gates[:, third:], first_tables[:, GATES, third:])
+        nc.scalar.copy(first_gates[:, :third], first_tables[:, GATES, :third])
+        nc.vector.tensor_copy(first_values[:], first_tables[:, VALUES])
+
+        first_product = held.tile([P, picked], F32, name="first_product")
+        first_gate = held.tile([P, picked], F32, name="first_gate")
+        first_result = held.tile([P, picked], F32, name="first_result", align_bytes=BURST)
+        nc.vector.tensor_tensor(first_product[:], first_values[:].indirect(offsets[:]), stream[:, 0], MULT)
+        nc.scalar.activation(first_gate[:], first_gates[:].indirect(offsets[:]), TANH)
+        nc.vector.tensor_tensor(first_result[:], first_product[:], first_gate[:], MULT)
+        nc.sync.dma_start(out_rows[0], first_result[:])
 
         cut = 5 * picked // 8
-        pieces = [(0, 0, picked), (1, 0, cut), (1, cut, picked)]
-        lists = [offsets[:, first // GROUP : last // GROUP] for b, first, last in pieces]
-        gate_tiles = [
-            held.tile([P, picked], F32, name="gate0"),
-            reused.tile([P, cut], F32, name="gate1", offset=0),
-            reused.tile([P, picked - cut], F32, name="gate2", offset=picked * 4),
-        ]
-        gated_tiles = [
-            held.tile([P, picked], F32, name="gated0"),
-            held.tile([P, cut], F32, name="gated1"),
-            reused.tile([P, picked - cut], F32, name="gated2", offset=0),
-        ]
-        results = [held.tile([P, picked], F32, name=f"result{b}", align_bytes=BURST) for b in range(blocks)]
-
-        def gate_stream(n):
-            b, first, last = pieces[n]
-            nc.scalar.activation(gate_tiles[n][:], gates[b][:].indirect(lists[n]), TANH)
-            nc.vector.tensor_tensor(gated_tiles[n][:], stream[:, b, first:last], gate_tiles[n][:], MULT)
-
-        def look_up(n):
-            b, first, last = pieces[n]
-            nc.vector.tensor_tensor(results[b][:, first:last], values[b][:].indirect(lists[n]), gated_tiles[n][:], MULT)
-            nc.sync.dma_start(out_rows[b, :, first:last], results[b][:, first:last])
-
-        gate_stream(0)
-        look_up(0)
-        gate_stream(1)
-        gate_stream(2)
-        look_up(1)
-        look_up(2)
+        pieces = [(0, cut), (cut, picked)]
+        lists = [offsets[:, first // GROUP : last // GROUP] for first, last in pieces]
+        gate_tiles = [reused.tile([P, cut], F32, name="gate0", offset=0), held.tile([P, picked - cut], F32, name="gate1")]
+        gated_tiles = [held.tile([P, cut], F32, name="gated0"), reused.tile([P, picked - cut], F32, name="gated1", offset=0)]
+        last_result = held.tile([P, picked], F32, name="last_result", align_bytes=BURST)
+        for n, (first, last) in enumerate(pieces):
+            nc.scalar.activation(gate_tiles[n][:], last_gates[:].indirect(lists[n]), TANH)
+            nc.vector.tensor_tensor(gated_tiles[n][:], stream[:, 1, first:last], gate_tiles[n][:], MULT)
+        for n, (first, last) in enumerate(pieces):
+            nc.vector.tensor_tensor(last_result[:, first:last], last_values[:].indirect(lists[n]), gated_tiles[n][:], MULT)
+            nc.sync.dma_start(out_rows[1, :, first:last], last_result[:, first:last])

@@ -19,7 +19,7 @@ def tile_lookup_vg_multanh_out_kernel(tc, tab, y, offs, out):
     out_rows = out.rearrange("(p b) v -> b p v", b=blocks)
 
     with tc.tile_pool(name="held", bufs=1) as held, tc.tile_pool(name="reused", bufs=1) as reused:
-        offsets = held.tile([P, picked // GROUP], U16, name="offsets")
+        offsets = held.tile([P, picked // GROUP], U16, name="offsets", align_bytes=BURST)
         first_tables = held.tile([P, 2, places], F32, name="first_tables", align_bytes=BURST)
         stream = held.tile([P, blocks, picked], F32, name="stream", align_bytes=BURST)
         last_gates = held.tile([P, places], F32, name="last_gates", align_bytes=BURST)

import concourse.mybir as mybir

F32, U16 = mybir.dt.float32, mybir.dt.uint16
MULT = mybir.AluOpType.mult
TANH = mybir.ActivationFunctionType.Tanh
P = 128
GROUP = 16
BURST = 256
VALUES, GATES = 0, 1


def tile_lookup_vg_multanh_out_kernel(tc, tab, y, offs, out):
    nc = tc.nc
    rows, picked = y.shape
    places = tab.shape[2]
    blocks = rows // P
    table_rows = tab.rearrange("t (p b) s -> b p t s", b=blocks)
    stream_rows = y.rearrange("(p b) v -> p b v", b=blocks)
    out_rows = out.rearrange("(p b) v -> b p v", b=blocks)

    with tc.tile_pool(name="held", bufs=1) as held, tc.tile_pool(name="reused", bufs=1) as reused:
        offsets = held.tile([P, picked // GROUP], U16, name="offsets", align_bytes=BURST)
        first_tables = held.tile([P, 2, places], F32, name="first_tables", align_bytes=BURST)
        stream = held.tile([P, blocks, picked], F32, name="stream", align_bytes=BURST)
        last_gates = held.tile([P, places], F32, name="last_gates", align_bytes=BURST)
        last_values = held.tile([P, places], F32, name="last_values", align_bytes=BURST)

        nc.sync.dma_start(first_tables[:], table_rows[0])
        nc.sync.dma_start(offsets[:], offs)
        nc.sync.dma_start(stream[:], stream_rows)
        nc.sync.dma_start(last_gates[:], table_rows[1, :, GATES])
        nc.sync.dma_start(last_values[:], table_rows[1, :, VALUES])

        first_values = held.tile([P, places], F32, name="first_values")
        first_gates = held.tile([P, places], F32, name="first_gates")
        third = 11 * places // 32
        nc.vector.tensor_copy(first_gates[:, third:], first_tables[:, GATES, third:])
        nc.scalar.copy(first_gates[:, :third], first_tables[:, GATES, :third])
        nc.vector.tensor_copy(first_values[:], first_tables[:, VALUES])

        first_product = held.tile([P, picked], F32, name="first_product")
        first_gate = held.tile([P, picked], F32, name="first_gate")
        first_result = held.tile([P, picked], F32, name="first_result", align_bytes=BURST)
        nc.vector.tensor_tensor(first_product[:], first_values[:].indirect(offsets[:]), stream[:, 0], MULT)
        nc.scalar.activation(first_gate[:], first_gates[:].indirect(offsets[:]), TANH)
        nc.vector.tensor_tensor(first_result[:], first_product[:], first_gate[:], MULT)
        nc.sync.dma_start(out_rows[0], first_result[:])

        cut = 5 * picked // 8
        pieces = [(0, cut), (cut, picked)]
        lists = [offsets[:, first // GROUP : last // GROUP] for first, last in pieces]
        gate_tiles = [reused.tile([P, cut], F32, name="gate0", offset=0), held.tile([P, picked - cut], F32, name="gate1")]
        gated_tiles = [held.tile([P, cut], F32, name="gated0"), reused.tile([P, picked - cut], F32, name="gated1", offset=0)]
        last_result = held.tile([P, picked], F32, name="last_result", align_bytes=BURST)
        for n, (first, last) in enumerate(pieces):
            nc.scalar.activation(gate_tiles[n][:], last_gates[:].indirect(lists[n]), TANH)
            nc.vector.tensor_tensor(gated_tiles[n][:], stream[:, 1, first:last], gate_tiles[n][:], MULT)
        for n, (first, last) in enumerate(pieces):
            nc.vector.tensor_tensor(last_result[:, first:last], last_values[:].indirect(lists[n]), gated_tiles[n][:], MULT)
            nc.sync.dma_start(out_rows[1, :, first:last], last_result[:, first:last])
